import numpy as np
import ml_dtypes


def mxq(x, axis, fmt="e4m3"):
    dtype, down = {"e4m3": (ml_dtypes.float8_e4m3fn, 7), "e5m2": (ml_dtypes.float8_e5m2, 14)}[fmt]
    v = np.moveaxis(np.asarray(x, np.float32).astype(ml_dtypes.bfloat16).astype(np.float64), axis, -1)
    blocks = v.reshape(v.shape[:-1] + (-1, 32))
    amax = np.abs(blocks).max(-1, keepdims=True)
    byte = np.maximum(np.where(amax > 0, np.frexp(amax)[1] - 1 + 127, 0) - down, 1)
    scale = np.exp2(byte - 127.0)
    codes = (blocks / scale).astype(np.float32).astype(dtype).astype(np.float64)
    return np.moveaxis((codes * scale).reshape(v.shape), -1, axis)


WIDE = False


def mx_kscale(k):
    if not WIDE:
        return np.ones(k)
    levels = np.array([10, -10, 5, -5, 0])
    if k % 512:
        return np.exp2(np.random.permutation(np.resize(levels, k // 32))).repeat(32)
    a = np.empty((k // 512, 16))
    for p in range(k // 512):
        a[p, :8] = np.random.permutation(np.resize(levels, 8))
        for g in range(8):
            far = levels[np.abs(levels - a[p, g]) >= 10]
            a[p, g + 8] = far[np.random.randint(len(far))]
    return np.exp2(a.ravel()).repeat(32)


def f64(x):
    return np.asarray(x).astype(np.float64)


def striped(idx):
    return np.tile(idx.reshape(-1, 16).T, (8, 1)).astype(np.uint16)


def unstriped(offs):
    return offs[:16].T.reshape(-1).astype(np.int64)


def pack_weight(w):
    k, n = w.shape
    w = f64(np.asarray(w, np.float32).astype(ml_dtypes.bfloat16)).reshape(k // 32, 32, n)
    amax = np.abs(w).max(1)
    byte = np.clip(np.where(amax > 0, np.frexp(amax)[1] - 1 + 127 - 7, 1), 1, 254)
    scaled = (w * np.exp2(127.0 - byte)[:, None, :]).reshape(k, n).astype(np.float32)
    words = np.ascontiguousarray(scaled.reshape(k // 512, 128, 4, n).transpose(0, 1, 3, 2)).astype(ml_dtypes.float8_e4m3fn).view(np.uint8)
    return words, np.ascontiguousarray(byte.astype(np.uint8).reshape(k // 512, 16, n))


def unpack_weight(words, scales):
    g, p, n, _ = words.shape
    vals = np.ascontiguousarray(words).view(ml_dtypes.float8_e4m3fn).astype(np.float64) * np.repeat(np.exp2(scales.astype(np.float64) - 127.0), 8, axis=1)[..., None]
    return vals.transpose(0, 1, 3, 2).reshape(g * 512, n)


K, T, D, S, V, N = 512, 1024, 6, 3072, 512, 256


def setup_inputs():
    n = np.random.standard_normal
    s = mx_kscale(K)[:, None]
    words, scales = pack_weight(n((K, N)) / np.sqrt(K) / s)
    return {
        "xT": (n((K, T)) * s).astype(np.float32),
        "w_words": words,
        "w_scales": scales,
        "gate": np.tile(np.random.uniform(0.2, 1.0, (D, 1, V)) / np.sqrt(D), (1, N, 1)).astype(np.float32),
        "pos1": striped(np.random.permutation(T)[:V]),
        "pos2": striped(np.random.permutation(T)[:V]),
        "pos3": striped(np.random.permutation(T)[:V]),
        "pos4": striped(np.random.permutation(T)[:V]),
        "pos5": striped(np.random.permutation(T)[:V]),
        "pos6": striped(np.random.permutation(T)[:V]),
    }


def reference(xT, w_words, w_scales, gate, pos1, pos2, pos3, pos4, pos5, pos6):
    w = unpack_weight(w_words, w_scales)
    y = w.T @ mxq(f64(xT), 0, "e4m3")
    return sum(f64(gate[d]) * y[:, unstriped(p)] for d, p in enumerate((pos1, pos2, pos3, pos4, pos5, pos6)))

@@ -1,0 +1,152 @@
+from contextlib import ExitStack
+
+import concourse.mybir as mybir
+from concourse.masks import make_identity
+
+K, T, D, V, N = 512, 1024, 6, 512, 256
+P = 128
+FLOPS = 2 * K * T * N + 2 * D * N * V
+
+F32 = mybir.dt.float32
+BF16 = mybir.dt.bfloat16
+U32 = mybir.dt.uint32
+I32 = mybir.dt.int32
+U16 = mybir.dt.uint16
+U8 = mybir.dt.uint8
+FP8X4 = mybir.dt.float8_e4m3fn_x4
+MULT = mybir.AluOpType.mult
+ADD = mybir.AluOpType.add
+
+CHUNKS = ((0, 256), (256, 256), (512, 256), (768, 256))
+SCALAR_COLS = 64
+
+
+def tile_picked_agg_lin_none_sub_l_kernel(
+    tc, xT, w_words, w_scales, gate, pos1, pos2, pos3, pos4, pos5, pos6, out
+):
+    nc = tc.nc
+    with ExitStack() as ctx:
+        held = ctx.enter_context(tc.tile_pool(name="held", bufs=1))
+        ring = ctx.enter_context(tc.tile_pool(name="ring", bufs=6))
+        psum = ctx.enter_context(tc.psum_pool(name="psum", bufs=1))
+
+        def bank(tag):
+            return psum.tile([P, 512], F32, name=f"bank_{tag}", tag=f"bank_{tag}")
+
+        w_sc = held.tile([P, N], U8, name="w_sc", align_bytes=64)
+        nc.vector.memset(w_sc[:].bitcast(I32), 0)
+        w_codes = held.tile([P, 4 * N], U8, name="w_codes", align_bytes=64)
+        ident = held.tile([P, P], F32, name="ident", align_bytes=64)
+        make_identity(nc, ident[:])
+
+        rows = xT.rearrange("(p t) n -> p t n", t=4)
+        raws = []
+        for c, (c0, width) in enumerate(CHUNKS):
+            raw = held.tile([P, 4, width], F32, name=f"raw{c}")
+            nc.sync.dma_start(out=raw[:], in_=rows[:, :, c0 : c0 + width])
+            raws.append(raw)
+        nc.scalar.dma_start(out=w_codes[:].bitcast(I32), in_=w_words[0].rearrange("p n t -> p (n t)").bitcast(I32))
+        for q in range(4):
+            nc.scalar.dma_start(
+                out=w_sc[32 * q : 32 * q + 4, :].bitcast(I32), in_=w_scales[0, 4 * q : 4 * q + 4, :].bitcast(I32)
+            )
+        lists = []
+        gates = [held.tile([P, D, V], F32, name=f"gate{b}") for b in range(2)]
+        for d, pos in enumerate((pos1, pos2, pos3, pos4, pos5, pos6)):
+            lst = held.tile([P, V // 16], U16, name=f"list{d}")
+            nc.sync.dma_start(lst[:], pos)
+            lists.append(lst)
+            nc.sync.dma_start(out=gates[0][:, d, :], in_=gate[d, 0:P, :])
+        for d0 in (0, 3):
+            nc.sync.dma_start(
+                out=gates[1][:, d0 : d0 + 3, :], in_=gate[d0 : d0 + 3, P : 2 * P, :].rearrange("d m v -> m d v")
+            )
+
+        codes = held.tile([P, T], U32, name="codes", align_bytes=64)
+        scales = held.tile([P, T], U8, name="scales", align_bytes=64)
+        y = [held.tile([P, T], F32, name=f"y{b}") for b in range(2)]
+        for c, (c0, width) in enumerate(CHUNKS):
+            grouped = held.tile([P, width, 4], BF16, name=f"grouped{c}", align_bytes=64)
+            cut = width - SCALAR_COLS
+            src = raws[c][:].rearrange("p t (c i) -> p c t i", i=4)
+            dst = grouped[:].rearrange("p (c i) t -> p c t i", i=4)
+            nc.vector.tensor_copy(out=dst[:, : cut // 4], in_=src[:, : cut // 4])
+            nc.scalar.copy(out=dst[:, cut // 4 :], in_=src[:, cut // 4 :])
+            cols = slice(c0, c0 + width)
+            nc.vector.quantize_mx(
+                out=codes[:, cols].bitcast(FP8X4), scales=scales[:, cols], in_=grouped[:].rearrange("p n t -> p (n t)")
+            )
+            acc = bank(c)
+            nc.tensor.matmul_mx(
+                out=acc[:, :width],
+                lhsT=w_codes[:, : 4 * P].bitcast(FP8X4),
+                lhsT_scale=w_sc[:, :P],
+                rhs=codes[:, cols].bitcast(FP8X4),
+                rhs_scale=scales[:, cols],
+                start=True,
+                stop=True,
+            )
+            nc.scalar.copy(out=y[0][:, cols], in_=acc[:, :width])
+        for h in range(2):
+            cols = slice(512 * h, 512 * h + 512)
+            acc = bank(4 + h)
+            nc.tensor.matmul_mx(
+                out=acc[:],
+                lhsT=w_codes[:, 4 * P :].bitcast(FP8X4),
+                lhsT_scale=w_sc[:, P:],
+                rhs=codes[:, cols].bitcast(FP8X4),
+                rhs_scale=scales[:, cols],
+                start=True,
+                stop=True,
+            )
+            nc.scalar.copy(out=y[1][:, cols], in_=acc[:])
+
+        def add_turned(accs, j, product, first, last):
+            nc.tensor.matmul(accs[j][:, :P], product, ident[:], start=first, stop=last, is_transpose=True)
+
+        accs = [bank(k) for k in (6, 7, 0, 1)]
+        for d in range(D):
+            prod = ring.tile([P, V], F32, name="prod")
+            nc.vector.tensor_tensor(prod[:], y[0][:].indirect(lists[d][:]), gates[0][:, d, :], MULT)
+            for j in range(4):
+                add_turned(accs, j, prod[:, P * j : P * (j + 1)], d == 0, d == D - 1)
+        turned = held.tile([P, 4, P], F32, name="turned0")
+        back = bank(2)
+        for j in range(4):
+            nc.scalar.copy(out=turned[:, j, :], in_=accs[j][:, :P])
+            nc.tensor.transpose(back[:, P * j : P * (j + 1)], turned[:, j, :], ident[:])
+        res = held.tile([P, V], F32, name="res0")
+        nc.scalar.copy(out=res[:], in_=back[:])
+        nc.sync.dma_start(out=out[0:P, :], in_=res[:])
+
+        accs = [bank(k) for k in (3, 4, 5, 6)]
+        for d in range(D - 2):
+            prod = ring.tile([P, V], F32, name="prod")
+            nc.vector.tensor_tensor(prod[:], y[1][:].indirect(lists[d][:]), gates[1][:, d, :], MULT)
+            for j in range(4):
+                add_turned(accs, j, prod[:, P * j : P * (j + 1)], d == 0, False)
+        H = V // 2
+        lasts = []
+        for d in (D - 2, D - 1):
+            for h in range(2):
+                prod = held.tile([P, H], F32, name=f"half{d}{h}")
+                nc.vector.tensor_tensor(
+                    prod[:],
+                    y[1][:].indirect(lists[d][:, 16 * h : 16 * h + 16]),
+                    gates[1][:, d, H * h : H * (h + 1)],
+                    MULT,
+                )
+                if d == D - 2:
+                    for j in range(2):
+                        add_turned(accs, 2 * h + j, prod[:, P * j : P * (j + 1)], False, True)
+                else:
+                    lasts.append(prod)
+        turned1 = held.tile([P, 4, P], F32, name="turned1")
+        for h in range(2):
+            back = bank((7, 0)[h])
+            for j in range(2):
+                nc.scalar.copy(out=turned1[:, 2 * h + j, :], in_=accs[2 * h + j][:, :P])
+                nc.tensor.transpose(back[:, P * j : P * (j + 1)], turned1[:, 2 * h + j, :], ident[:])
+            res = held.tile([P, H], F32, name=f"res1{h}")
+            nc.vector.tensor_tensor(res[:], back[:, :H], lasts[h][:], ADD)
+            nc.sync.dma_start(out=out[P : 2 * P, H * h : H * (h + 1)], in_=res[:])

@@ -17,8 +17,7 @@ FP8X4 = mybir.dt.float8_e4m3fn_x4
 MULT = mybir.AluOpType.mult
 ADD = mybir.AluOpType.add
 
-CHUNKS = ((0, 256), (256, 256), (512, 256), (768, 256))
-SCALAR_COLS = 64
+CHUNKS = ((0, 256, 96), (256, 256, 96), (512, 256, 96), (768, 128, 32), (896, 128, 32))
 
 
 def tile_picked_agg_lin_none_sub_l_kernel(
@@ -41,7 +40,7 @@ def tile_picked_agg_lin_none_sub_l_kernel(
 
         rows = xT.rearrange("(p t) n -> p t n", t=4)
         raws = []
-        for c, (c0, width) in enumerate(CHUNKS):
+        for c, (c0, width, scalar_cols) in enumerate(CHUNKS):
             raw = held.tile([P, 4, width], F32, name=f"raw{c}")
             nc.sync.dma_start(out=raw[:], in_=rows[:, :, c0 : c0 + width])
             raws.append(raw)
@@ -56,7 +55,9 @@ def tile_picked_agg_lin_none_sub_l_kernel(
             lst = held.tile([P, V // 16], U16, name=f"list{d}")
             nc.sync.dma_start(lst[:], pos)
             lists.append(lst)
-            nc.sync.dma_start(out=gates[0][:, d, :], in_=gate[d, 0:P, :])
+            if d in (0, 2, 5):
+                d0 = {0: 0, 2: 1, 5: 3}[d]
+                nc.sync.dma_start(out=gates[0][:, d0 : d + 1, :], in_=gate[d0 : d + 1, 0:P, :].rearrange("d m v -> m d v"))
         for d0 in (0, 3):
             nc.sync.dma_start(
                 out=gates[1][:, d0 : d0 + 3, :], in_=gate[d0 : d0 + 3, P : 2 * P, :].rearrange("d m v -> m d v")
@@ -65,9 +66,9 @@ def tile_picked_agg_lin_none_sub_l_kernel(
         codes = held.tile([P, T], U32, name="codes", align_bytes=64)
         scales = held.tile([P, T], U8, name="scales", align_bytes=64)
         y = [held.tile([P, T], F32, name=f"y{b}") for b in range(2)]
-        for c, (c0, width) in enumerate(CHUNKS):
+        for c, (c0, width, scalar_cols) in enumerate(CHUNKS):
             grouped = held.tile([P, width, 4], BF16, name=f"grouped{c}", align_bytes=64)
-            cut = width - SCALAR_COLS
+            cut = width - scalar_cols
             src = raws[c][:].rearrange("p t (c i) -> p c t i", i=4)
             dst = grouped[:].rearrange("p (c i) t -> p c t i", i=4)
             nc.vector.tensor_copy(out=dst[:, : cut // 4], in_=src[:, : cut // 4])
@@ -89,7 +90,7 @@ def tile_picked_agg_lin_none_sub_l_kernel(
             nc.scalar.copy(out=y[0][:, cols], in_=acc[:, :width])
         for h in range(2):
             cols = slice(512 * h, 512 * h + 512)
-            acc = bank(4 + h)
+            acc = bank(5 + h)
             nc.tensor.matmul_mx(
                 out=acc[:],
                 lhsT=w_codes[:, 4 * P :].bitcast(FP8X4),
@@ -104,14 +105,14 @@ def tile_picked_agg_lin_none_sub_l_kernel(
         def add_turned(accs, j, product, first, last):
             nc.tensor.matmul(accs[j][:, :P], product, ident[:], start=first, stop=last, is_transpose=True)
 
-        accs = [bank(k) for k in (6, 7, 0, 1)]
+        accs = [bank(k) for k in (7, 0, 1, 2)]
         for d in range(D):
             prod = ring.tile([P, V], F32, name="prod")
             nc.vector.tensor_tensor(prod[:], y[0][:].indirect(lists[d][:]), gates[0][:, d, :], MULT)
             for j in range(4):
                 add_turned(accs, j, prod[:, P * j : P * (j + 1)], d == 0, d == D - 1)
         turned = held.tile([P, 4, P], F32, name="turned0")
-        back = bank(2)
+        back = bank(3)
         for j in range(4):
             nc.scalar.copy(out=turned[:, j, :], in_=accs[j][:, :P])
             nc.tensor.transpose(back[:, P * j : P * (j + 1)], turned[:, j, :], ident[:])
@@ -119,31 +120,26 @@ def tile_picked_agg_lin_none_sub_l_kernel(
         nc.scalar.copy(out=res[:], in_=back[:])
         nc.sync.dma_start(out=out[0:P, :], in_=res[:])
 
-        accs = [bank(k) for k in (3, 4, 5, 6)]
-        for d in range(D - 2):
+        accs = [bank(k) for k in (4, 5, 6, 7)]
+        for d in range(D - 1):
             prod = ring.tile([P, V], F32, name="prod")
             nc.vector.tensor_tensor(prod[:], y[1][:].indirect(lists[d][:]), gates[1][:, d, :], MULT)
             for j in range(4):
-                add_turned(accs, j, prod[:, P * j : P * (j + 1)], d == 0, False)
+                add_turned(accs, j, prod[:, P * j : P * (j + 1)], d == 0, d == D - 2)
         H = V // 2
         lasts = []
-        for d in (D - 2, D - 1):
-            for h in range(2):
-                prod = held.tile([P, H], F32, name=f"half{d}{h}")
-                nc.vector.tensor_tensor(
-                    prod[:],
-                    y[1][:].indirect(lists[d][:, 16 * h : 16 * h + 16]),
-                    gates[1][:, d, H * h : H * (h + 1)],
-                    MULT,
-                )
-                if d == D - 2:
-                    for j in range(2):
-                        add_turned(accs, 2 * h + j, prod[:, P * j : P * (j + 1)], False, True)
-                else:
-                    lasts.append(prod)
+        for h in range(2):
+            prod = held.tile([P, H], F32, name=f"last{h}")
+            nc.vector.tensor_tensor(
+                prod[:],
+                y[1][:].indirect(lists[D - 1][:, 16 * h : 16 * h + 16]),
+                gates[1][:, D - 1, H * h : H * (h + 1)],
+                MULT,
+            )
+            lasts.append(prod)
         turned1 = held.tile([P, 4, P], F32, name="turned1")
         for h in range(2):
-            back = bank((7, 0)[h])
+            back = bank(h)
             for j in range(2):
                 nc.scalar.copy(out=turned1[:, 2 * h + j, :], in_=accs[2 * h + j][:, :P])
                 nc.tensor.transpose(back[:, P * j : P * (j + 1)], turned1[:, 2 * h + j, :], ident[:])

@@ -17,7 +17,7 @@ FP8X4 = mybir.dt.float8_e4m3fn_x4
 MULT = mybir.AluOpType.mult
 ADD = mybir.AluOpType.add
 
-CHUNKS = ((0, 256, 96), (256, 256, 96), (512, 256, 96), (768, 128, 32), (896, 128, 32))
+LOADS = (((256, 96), (256, 96)), ((256, 96),), ((128, 0), (128, 64)))
 
 
 def tile_picked_agg_lin_none_sub_l_kernel(
@@ -29,90 +29,117 @@ def tile_picked_agg_lin_none_sub_l_kernel(
         ring = ctx.enter_context(tc.tile_pool(name="ring", bufs=6))
         psum = ctx.enter_context(tc.psum_pool(name="psum", bufs=1))
 
-        def bank(tag):
-            return psum.tile([P, 512], F32, name=f"bank_{tag}", tag=f"bank_{tag}")
+        def bank(k):
+            return psum.tile([P, 512], F32, name=f"bank{k}", tag=f"bank{k}")
 
         w_sc = held.tile([P, N], U8, name="w_sc", align_bytes=64)
-        nc.vector.memset(w_sc[:].bitcast(I32), 0)
+        nc.gpsimd.memset(w_sc[:].bitcast(I32), 0)
         w_codes = held.tile([P, 4 * N], U8, name="w_codes", align_bytes=64)
-        ident = held.tile([P, P], F32, name="ident", align_bytes=64)
-        make_identity(nc, ident[:])
-
-        rows = xT.rearrange("(p t) n -> p t n", t=4)
-        raws = []
-        for c, (c0, width, scalar_cols) in enumerate(CHUNKS):
-            raw = held.tile([P, 4, width], F32, name=f"raw{c}")
-            nc.sync.dma_start(out=raw[:], in_=rows[:, :, c0 : c0 + width])
-            raws.append(raw)
         nc.scalar.dma_start(out=w_codes[:].bitcast(I32), in_=w_words[0].rearrange("p n t -> p (n t)").bitcast(I32))
         for q in range(4):
             nc.scalar.dma_start(
                 out=w_sc[32 * q : 32 * q + 4, :].bitcast(I32), in_=w_scales[0, 4 * q : 4 * q + 4, :].bitcast(I32)
             )
+        ident = held.tile([P, P], F32, name="ident", align_bytes=64)
+        make_identity(nc, ident[:])
+
+        rows = xT.rearrange("(p t) n -> p t n", t=4)
+        raws = []
+        c0 = 0
+        for c, pieces in enumerate(LOADS):
+            width = sum(piece[0] for piece in pieces)
+            raw = held.tile([P, 4, width], F32, name=f"raw{c}")
+            nc.sync.dma_start(out=raw[:], in_=rows[:, :, c0 : c0 + width])
+            raws.append(raw)
+            c0 += width
         lists = []
         gates = [held.tile([P, D, V], F32, name=f"gate{b}") for b in range(2)]
+
+        def load_gates(b, d0, d1):
+            nc.sync.dma_start(
+                out=gates[b][:, d0:d1, :], in_=gate[d0:d1, P * b : P * (b + 1), :].rearrange("d m v -> m d v")
+            )
+
         for d, pos in enumerate((pos1, pos2, pos3, pos4, pos5, pos6)):
             lst = held.tile([P, V // 16], U16, name=f"list{d}")
             nc.sync.dma_start(lst[:], pos)
             lists.append(lst)
-            if d in (0, 2, 5):
-                d0 = {0: 0, 2: 1, 5: 3}[d]
-                nc.sync.dma_start(out=gates[0][:, d0 : d + 1, :], in_=gate[d0 : d + 1, 0:P, :].rearrange("d m v -> m d v"))
-        for d0 in (0, 3):
-            nc.sync.dma_start(
-                out=gates[1][:, d0 : d0 + 3, :], in_=gate[d0 : d0 + 3, P : 2 * P, :].rearrange("d m v -> m d v")
-            )
+            if d == 0:
+                load_gates(0, 0, 1)
+            if d == 2:
+                load_gates(0, 1, 3)
+            if d == 5:
+                load_gates(0, 3, 6)
+        load_gates(1, 0, 3)
+        load_gates(1, 3, 6)
 
         codes = held.tile([P, T], U32, name="codes", align_bytes=64)
         scales = held.tile([P, T], U8, name="scales", align_bytes=64)
         y = [held.tile([P, T], F32, name=f"y{b}") for b in range(2)]
-        for c, (c0, width, scalar_cols) in enumerate(CHUNKS):
-            grouped = held.tile([P, width, 4], BF16, name=f"grouped{c}", align_bytes=64)
-            cut = width - scalar_cols
-            src = raws[c][:].rearrange("p t (c i) -> p c t i", i=4)
-            dst = grouped[:].rearrange("p (c i) t -> p c t i", i=4)
-            nc.vector.tensor_copy(out=dst[:, : cut // 4], in_=src[:, : cut // 4])
-            nc.scalar.copy(out=dst[:, cut // 4 :], in_=src[:, cut // 4 :])
-            cols = slice(c0, c0 + width)
-            nc.vector.quantize_mx(
-                out=codes[:, cols].bitcast(FP8X4), scales=scales[:, cols], in_=grouped[:].rearrange("p n t -> p (n t)")
+
+        def project(acc_ap, b, cols):
+            nc.tensor.matmul_mx(
+                out=acc_ap,
+                lhsT=w_codes[:, 4 * P * b : 4 * P * (b + 1)].bitcast(FP8X4),
+                lhsT_scale=w_sc[:, P * b : P * (b + 1)],
+                rhs=codes[:, cols].bitcast(FP8X4),
+                rhs_scale=scales[:, cols],
+                start=True,
+                stop=True,
             )
+
+        c0 = 0
+        copies = []
+        for c, pieces in enumerate(LOADS):
+            grouped = []
+            r0 = 0
+            for i, (width, scalar_cols) in enumerate(pieces):
+                tile = held.tile([P, width, 4], BF16, name=f"grouped{c}_{i}", align_bytes=64)
+                cut = (width - scalar_cols) // 4
+                src = raws[c][:, :, r0 : r0 + width].rearrange("p t (c i) -> p c t i", i=4)
+                dst = tile[:].rearrange("p (c i) t -> p c t i", i=4)
+                nc.vector.tensor_copy(out=dst[:, :cut], in_=src[:, :cut])
+                if scalar_cols > 0:
+                    nc.scalar.copy(out=dst[:, cut:], in_=src[:, cut:])
+                grouped.append(tile)
+                r0 += width
             acc = bank(c)
-            nc.tensor.matmul_mx(
-                out=acc[:, :width],
-                lhsT=w_codes[:, : 4 * P].bitcast(FP8X4),
-                lhsT_scale=w_sc[:, :P],
-                rhs=codes[:, cols].bitcast(FP8X4),
-                rhs_scale=scales[:, cols],
-                start=True,
-                stop=True,
-            )
-            nc.scalar.copy(out=y[0][:, cols], in_=acc[:, :width])
+            r0 = 0
+            for (width, scalar_cols), tile in zip(pieces, grouped):
+                cols = slice(c0 + r0, c0 + r0 + width)
+                nc.vector.quantize_mx(
+                    out=codes[:, cols].bitcast(FP8X4), scales=scales[:, cols], in_=tile[:].rearrange("p n t -> p (n t)")
+                )
+                project(acc[:, r0 : r0 + width], 0, cols)
+                r0 += width
+            copies.append((y[0][:, c0 : c0 + r0], acc[:, :r0]))
+            if c > 0:
+                nc.scalar.copy(out=copies[c - 1][0], in_=copies[c - 1][1])
+            c0 += r0
+        nc.scalar.copy(out=copies[-1][0], in_=copies[-1][1])
         for h in range(2):
-            cols = slice(512 * h, 512 * h + 512)
-            acc = bank(5 + h)
-            nc.tensor.matmul_mx(
-                out=acc[:],
-                lhsT=w_codes[:, 4 * P :].bitcast(FP8X4),
-                lhsT_scale=w_sc[:, P:],
-                rhs=codes[:, cols].bitcast(FP8X4),
-                rhs_scale=scales[:, cols],
-                start=True,
-                stop=True,
-            )
+            cols = slice(512 * h, 512 * (h + 1))
+            acc = bank(3 + h)
+            project(acc[:], 1, cols)
             nc.scalar.copy(out=y[1][:, cols], in_=acc[:])
 
-        def add_turned(accs, j, product, first, last):
-            nc.tensor.matmul(accs[j][:, :P], product, ident[:], start=first, stop=last, is_transpose=True)
+        def product(b, d, h0, h1, pool, name):
+            prod = pool.tile([P, h1 - h0], F32, name=name)
+            whole = h1 - h0 == V
+            offsets = lists[d][:] if whole else lists[d][:, h0 // 16 : h1 // 16]
+            nc.vector.tensor_tensor(prod[:], y[b][:].indirect(offsets), gates[b][:, d, h0:h1], MULT)
+            return prod
 
-        accs = [bank(k) for k in (7, 0, 1, 2)]
+        def add_turned(acc, piece, first, last):
+            nc.tensor.matmul(acc[:, :P], piece, ident[:], start=first, stop=last, is_transpose=True)
+
+        accs = [bank(k) for k in (5, 6, 7, 0)]
         for d in range(D):
-            prod = ring.tile([P, V], F32, name="prod")
-            nc.vector.tensor_tensor(prod[:], y[0][:].indirect(lists[d][:]), gates[0][:, d, :], MULT)
+            prod = product(0, d, 0, V, ring, "prod")
             for j in range(4):
-                add_turned(accs, j, prod[:, P * j : P * (j + 1)], d == 0, d == D - 1)
+                add_turned(accs[j], prod[:, P * j : P * (j + 1)], d == 0, d == D - 1)
         turned = held.tile([P, 4, P], F32, name="turned0")
-        back = bank(3)
+        back = bank(1)
         for j in range(4):
             nc.scalar.copy(out=turned[:, j, :], in_=accs[j][:, :P])
             nc.tensor.transpose(back[:, P * j : P * (j + 1)], turned[:, j, :], ident[:])
@@ -120,29 +147,23 @@ def tile_picked_agg_lin_none_sub_l_kernel(
         nc.scalar.copy(out=res[:], in_=back[:])
         nc.sync.dma_start(out=out[0:P, :], in_=res[:])
 
-        accs = [bank(k) for k in (4, 5, 6, 7)]
-        for d in range(D - 1):
-            prod = ring.tile([P, V], F32, name="prod")
-            nc.vector.tensor_tensor(prod[:], y[1][:].indirect(lists[d][:]), gates[1][:, d, :], MULT)
-            for j in range(4):
-                add_turned(accs, j, prod[:, P * j : P * (j + 1)], d == 0, d == D - 2)
         H = V // 2
-        lasts = []
+        accs = [bank(k) for k in (2, 3, 4, 5)]
+        for d in range(D - 2):
+            prod = product(1, d, 0, V, ring, "prod")
+            for j in range(4):
+                add_turned(accs[j], prod[:, P * j : P * (j + 1)], d == 0, False)
         for h in range(2):
-            prod = held.tile([P, H], F32, name=f"last{h}")
-            nc.vector.tensor_tensor(
-                prod[:],
-                y[1][:].indirect(lists[D - 1][:, 16 * h : 16 * h + 16]),
-                gates[1][:, D - 1, H * h : H * (h + 1)],
-                MULT,
-            )
-            lasts.append(prod)
-        turned1 = held.tile([P, 4, P], F32, name="turned1")
-        for h in range(2):
-            back = bank(h)
+            prod = product(1, D - 2, H * h, H * (h + 1), held, f"fifth{h}")
             for j in range(2):
-                nc.scalar.copy(out=turned1[:, 2 * h + j, :], in_=accs[2 * h + j][:, :P])
-                nc.tensor.transpose(back[:, P * j : P * (j + 1)], turned1[:, 2 * h + j, :], ident[:])
-            res = held.tile([P, H], F32, name=f"res1{h}")
+                add_turned(accs[2 * h + j], prod[:, P * j : P * (j + 1)], False, True)
+        lasts = [product(1, D - 1, H * h, H * (h + 1), held, f"last{h}") for h in range(2)]
+        turned = held.tile([P, 4, P], F32, name="turned1")
+        for h in range(2):
+            back = bank(6 + h)
+            for j in range(2):
+                nc.scalar.copy(out=turned[:, 2 * h + j, :], in_=accs[2 * h + j][:, :P])
+                nc.tensor.transpose(back[:, P * j : P * (j + 1)], turned[:, 2 * h + j, :], ident[:])
+            res = held.tile([P, H], F32, name=f"res1_{h}")
             nc.vector.tensor_tensor(res[:], back[:, :H], lasts[h][:], ADD)
             nc.sync.dma_start(out=out[P : 2 * P, H * h : H * (h + 1)], in_=res[:])

@@ -17,7 +17,7 @@ FP8X4 = mybir.dt.float8_e4m3fn_x4
 MULT = mybir.AluOpType.mult
 ADD = mybir.AluOpType.add
 
-LOADS = (((256, 96), (256, 96)), ((256, 96),), ((128, 0), (128, 64)))
+CHUNKS = ((256, 128), (256, 128), (256, 96), (128, 32), (128, 0))
 
 
 def tile_picked_agg_lin_none_sub_l_kernel(
@@ -46,8 +46,7 @@ def tile_picked_agg_lin_none_sub_l_kernel(
         rows = xT.rearrange("(p t) n -> p t n", t=4)
         raws = []
         c0 = 0
-        for c, pieces in enumerate(LOADS):
-            width = sum(piece[0] for piece in pieces)
+        for c, (width, scalar_cols) in enumerate(CHUNKS):
             raw = held.tile([P, 4, width], F32, name=f"raw{c}")
             nc.sync.dma_start(out=raw[:], in_=rows[:, :, c0 : c0 + width])
             raws.append(raw)
@@ -90,36 +89,28 @@ def tile_picked_agg_lin_none_sub_l_kernel(
 
         c0 = 0
         copies = []
-        for c, pieces in enumerate(LOADS):
-            grouped = []
-            r0 = 0
-            for i, (width, scalar_cols) in enumerate(pieces):
-                tile = held.tile([P, width, 4], BF16, name=f"grouped{c}_{i}", align_bytes=64)
-                cut = (width - scalar_cols) // 4
-                src = raws[c][:, :, r0 : r0 + width].rearrange("p t (c i) -> p c t i", i=4)
-                dst = tile[:].rearrange("p (c i) t -> p c t i", i=4)
-                nc.vector.tensor_copy(out=dst[:, :cut], in_=src[:, :cut])
-                if scalar_cols > 0:
-                    nc.scalar.copy(out=dst[:, cut:], in_=src[:, cut:])
-                grouped.append(tile)
-                r0 += width
+        for c, (width, scalar_cols) in enumerate(CHUNKS):
+            grouped = held.tile([P, width, 4], BF16, name=f"grouped{c}", align_bytes=64)
+            cut = (width - scalar_cols) // 4
+            src = raws[c][:].rearrange("p t (c i) -> p c t i", i=4)
+            dst = grouped[:].rearrange("p (c i) t -> p c t i", i=4)
+            nc.vector.tensor_copy(out=dst[:, :cut], in_=src[:, :cut])
+            if scalar_cols > 0:
+                nc.scalar.copy(out=dst[:, cut:], in_=src[:, cut:])
+            cols = slice(c0, c0 + width)
+            nc.vector.quantize_mx(
+                out=codes[:, cols].bitcast(FP8X4), scales=scales[:, cols], in_=grouped[:].rearrange("p n t -> p (n t)")
+            )
             acc = bank(c)
-            r0 = 0
-            for (width, scalar_cols), tile in zip(pieces, grouped):
-                cols = slice(c0 + r0, c0 + r0 + width)
-                nc.vector.quantize_mx(
-                    out=codes[:, cols].bitcast(FP8X4), scales=scales[:, cols], in_=tile[:].rearrange("p n t -> p (n t)")
-                )
-                project(acc[:, r0 : r0 + width], 0, cols)
-                r0 += width
-            copies.append((y[0][:, c0 : c0 + r0], acc[:, :r0]))
+            project(acc[:, :width], 0, cols)
+            copies.append((y[0][:, cols], acc[:, :width]))
             if c > 0:
                 nc.scalar.copy(out=copies[c - 1][0], in_=copies[c - 1][1])
-            c0 += r0
+            c0 += width
         nc.scalar.copy(out=copies[-1][0], in_=copies[-1][1])
         for h in range(2):
             cols = slice(512 * h, 512 * (h + 1))
-            acc = bank(3 + h)
+            acc = bank(5 + h)
             project(acc[:], 1, cols)
             nc.scalar.copy(out=y[1][:, cols], in_=acc[:])
 
@@ -133,13 +124,13 @@ def tile_picked_agg_lin_none_sub_l_kernel(
         def add_turned(acc, piece, first, last):
             nc.tensor.matmul(acc[:, :P], piece, ident[:], start=first, stop=last, is_transpose=True)
 
-        accs = [bank(k) for k in (5, 6, 7, 0)]
+        accs = [bank(k) for k in (7, 0, 1, 2)]
         for d in range(D):
             prod = product(0, d, 0, V, ring, "prod")
             for j in range(4):
                 add_turned(accs[j], prod[:, P * j : P * (j + 1)], d == 0, d == D - 1)
         turned = held.tile([P, 4, P], F32, name="turned0")
-        back = bank(1)
+        back = bank(3)
         for j in range(4):
             nc.scalar.copy(out=turned[:, j, :], in_=accs[j][:, :P])
             nc.tensor.transpose(back[:, P * j : P * (j + 1)], turned[:, j, :], ident[:])
@@ -147,23 +138,23 @@ def tile_picked_agg_lin_none_sub_l_kernel(
         nc.scalar.copy(out=res[:], in_=back[:])
         nc.sync.dma_start(out=out[0:P, :], in_=res[:])
 
-        H = V // 2
-        accs = [bank(k) for k in (2, 3, 4, 5)]
+        parts = ((0, 384), (384, 512))
+        accs = [bank(k) for k in (4, 5, 6, 7)]
         for d in range(D - 2):
             prod = product(1, d, 0, V, ring, "prod")
             for j in range(4):
                 add_turned(accs[j], prod[:, P * j : P * (j + 1)], d == 0, False)
-        for h in range(2):
-            prod = product(1, D - 2, H * h, H * (h + 1), held, f"fifth{h}")
-            for j in range(2):
-                add_turned(accs[2 * h + j], prod[:, P * j : P * (j + 1)], False, True)
-        lasts = [product(1, D - 1, H * h, H * (h + 1), held, f"last{h}") for h in range(2)]
+        for h0, h1 in parts:
+            prod = product(1, D - 2, h0, h1, held, f"fifth{h0}")
+            for j in range(h0 // P, h1 // P):
+                add_turned(accs[j], prod[:, P * j - h0 : P * (j + 1) - h0], False, True)
+        lasts = [product(1, D - 1, h0, h1, held, f"last{h0}") for h0, h1 in parts]
         turned = held.tile([P, 4, P], F32, name="turned1")
-        for h in range(2):
-            back = bank(6 + h)
-            for j in range(2):
-                nc.scalar.copy(out=turned[:, 2 * h + j, :], in_=accs[2 * h + j][:, :P])
-                nc.tensor.transpose(back[:, P * j : P * (j + 1)], turned[:, 2 * h + j, :], ident[:])
-            res = held.tile([P, H], F32, name=f"res1_{h}")
-            nc.vector.tensor_tensor(res[:], back[:, :H], lasts[h][:], ADD)
-            nc.sync.dma_start(out=out[P : 2 * P, H * h : H * (h + 1)], in_=res[:])
+        for i, (h0, h1) in enumerate(parts):
+            back = bank(i)
+            for j in range(h0 // P, h1 // P):
+                nc.scalar.copy(out=turned[:, j, :], in_=accs[j][:, :P])
+                nc.tensor.transpose(back[:, P * j - h0 : P * (j + 1) - h0], turned[:, j, :], ident[:])
+            res = held.tile([P, h1 - h0], F32, name=f"res1_{h0}")
+            nc.vector.tensor_tensor(res[:], back[:, : h1 - h0], lasts[i][:], ADD)
+            nc.sync.dma_start(out=out[P : 2 * P, h0:h1], in_=res[:])

from contextlib import ExitStack

import concourse.mybir as mybir
from concourse.masks import make_identity

K, T, D, V, N = 512, 1024, 6, 512, 256
P = 128
FLOPS = 2 * K * T * N + 2 * D * N * V

F32 = mybir.dt.float32
BF16 = mybir.dt.bfloat16
U32 = mybir.dt.uint32
I32 = mybir.dt.int32
U16 = mybir.dt.uint16
U8 = mybir.dt.uint8
FP8X4 = mybir.dt.float8_e4m3fn_x4
MULT = mybir.AluOpType.mult
ADD = mybir.AluOpType.add

CHUNKS = ((256, 128), (256, 128), (256, 96), (128, 32), (128, 0))


def tile_picked_agg_lin_none_sub_l_kernel(
    tc, xT, w_words, w_scales, gate, pos1, pos2, pos3, pos4, pos5, pos6, out
):
    nc = tc.nc
    with ExitStack() as ctx:
        held = ctx.enter_context(tc.tile_pool(name="held", bufs=1))
        ring = ctx.enter_context(tc.tile_pool(name="ring", bufs=6))
        psum = ctx.enter_context(tc.psum_pool(name="psum", bufs=1))

        def bank(k):
            return psum.tile([P, 512], F32, name=f"bank{k}", tag=f"bank{k}")

        w_sc = held.tile([P, N], U8, name="w_sc", align_bytes=64)
        nc.gpsimd.memset(w_sc[:].bitcast(I32), 0)
        w_codes = held.tile([P, 4 * N], U8, name="w_codes", align_bytes=64)
        nc.scalar.dma_start(out=w_codes[:].bitcast(I32), in_=w_words[0].rearrange("p n t -> p (n t)").bitcast(I32))
        for q in range(4):
            nc.scalar.dma_start(
                out=w_sc[32 * q : 32 * q + 4, :].bitcast(I32), in_=w_scales[0, 4 * q : 4 * q + 4, :].bitcast(I32)
            )
        ident = held.tile([P, P], F32, name="ident", align_bytes=64)
        make_identity(nc, ident[:])

        rows = xT.rearrange("(p t) n -> p t n", t=4)
        raws = []
        c0 = 0
        for c, (width, scalar_cols) in enumerate(CHUNKS):
            raw = held.tile([P, 4, width], F32, name=f"raw{c}")
            nc.sync.dma_start(out=raw[:], in_=rows[:, :, c0 : c0 + width])
            raws.append(raw)
            c0 += width
        lists = []
        gates = [held.tile([P, D, V], F32, name=f"gate{b}") for b in range(2)]

        def load_gates(b, d0, d1):
            nc.sync.dma_start(
                out=gates[b][:, d0:d1, :], in_=gate[d0:d1, P * b : P * (b + 1), :].rearrange("d m v -> m d v")
            )

        for d, pos in enumerate((pos1, pos2, pos3, pos4, pos5, pos6)):
            lst = held.tile([P, V // 16], U16, name=f"list{d}")
            nc.sync.dma_start(lst[:], pos)
            lists.append(lst)
            if d == 0:
                load_gates(0, 0, 1)
            if d == 2:
                load_gates(0, 1, 3)
            if d == 5:
                load_gates(0, 3, 6)
        load_gates(1, 0, 3)
        load_gates(1, 3, 6)

        codes = held.tile([P, T], U32, name="codes", align_bytes=64)
        scales = held.tile([P, T], U8, name="scales", align_bytes=64)
        y = [held.tile([P, T], F32, name=f"y{b}") for b in range(2)]

        def project(acc_ap, b, cols):
            nc.tensor.matmul_mx(
                out=acc_ap,
                lhsT=w_codes[:, 4 * P * b : 4 * P * (b + 1)].bitcast(FP8X4),
                lhsT_scale=w_sc[:, P * b : P * (b + 1)],
                rhs=codes[:, cols].bitcast(FP8X4),
                rhs_scale=scales[:, cols],
                start=True,
                stop=True,
            )

        c0 = 0
        copies = []
        for c, (width, scalar_cols) in enumerate(CHUNKS):
            grouped = held.tile([P, width, 4], BF16, name=f"grouped{c}", align_bytes=64)
            cut = (width - scalar_cols) // 4
            src = raws[c][:].rearrange("p t (c i) -> p c t i", i=4)
            dst = grouped[:].rearrange("p (c i) t -> p c t i", i=4)
            nc.vector.tensor_copy(out=dst[:, :cut], in_=src[:, :cut])
            if scalar_cols > 0:
                nc.scalar.copy(out=dst[:, cut:], in_=src[:, cut:])
            cols = slice(c0, c0 + width)
            nc.vector.quantize_mx(
                out=codes[:, cols].bitcast(FP8X4), scales=scales[:, cols], in_=grouped[:].rearrange("p n t -> p (n t)")
            )
            acc = bank(c)
            project(acc[:, :width], 0, cols)
            copies.append((y[0][:, cols], acc[:, :width]))
            if c > 0:
                nc.scalar.copy(out=copies[c - 1][0], in_=copies[c - 1][1])
            c0 += width
        nc.scalar.copy(out=copies[-1][0], in_=copies[-1][1])
        for h in range(2):
            cols = slice(512 * h, 512 * (h + 1))
            acc = bank(5 + h)
            project(acc[:], 1, cols)
            nc.scalar.copy(out=y[1][:, cols], in_=acc[:])

        def product(b, d, h0, h1, pool, name):
            prod = pool.tile([P, h1 - h0], F32, name=name)
            whole = h1 - h0 == V
            offsets = lists[d][:] if whole else lists[d][:, h0 // 16 : h1 // 16]
            nc.vector.tensor_tensor(prod[:], y[b][:].indirect(offsets), gates[b][:, d, h0:h1], MULT)
            return prod

        def add_turned(acc, piece, first, last):
            nc.tensor.matmul(acc[:, :P], piece, ident[:], start=first, stop=last, is_transpose=True)

        accs = [bank(k) for k in (7, 0, 1, 2)]
        for d in range(D):
            prod = product(0, d, 0, V, ring, "prod")
            for j in range(4):
                add_turned(accs[j], prod[:, P * j : P * (j + 1)], d == 0, d == D - 1)
        turned = held.tile([P, 4, P], F32, name="turned0")
        back = bank(3)
        for j in range(4):
            nc.scalar.copy(out=turned[:, j, :], in_=accs[j][:, :P])
            nc.tensor.transpose(back[:, P * j : P * (j + 1)], turned[:, j, :], ident[:])
        res = held.tile([P, V], F32, name="res0")
        nc.scalar.copy(out=res[:], in_=back[:])
        nc.sync.dma_start(out=out[0:P, :], in_=res[:])

        parts = ((0, 384), (384, 512))
        accs = [bank(k) for k in (4, 5, 6, 7)]
        for d in range(D - 2):
            prod = product(1, d, 0, V, ring, "prod")
            for j in range(4):
                add_turned(accs[j], prod[:, P * j : P * (j + 1)], d == 0, False)
        for h0, h1 in parts:
            prod = product(1, D - 2, h0, h1, held, f"fifth{h0}")
            for j in range(h0 // P, h1 // P):
                add_turned(accs[j], prod[:, P * j - h0 : P * (j + 1) - h0], False, True)
        lasts = [product(1, D - 1, h0, h1, held, f"last{h0}") for h0, h1 in parts]
        turned = held.tile([P, 4, P], F32, name="turned1")
        for i, (h0, h1) in enumerate(parts):
            back = bank(i)
            for j in range(h0 // P, h1 // P):
                nc.scalar.copy(out=turned[:, j, :], in_=accs[j][:, :P])
                nc.tensor.transpose(back[:, P * j - h0 : P * (j + 1) - h0], turned[:, j, :], ident[:])
            res = held.tile([P, h1 - h0], F32, name=f"res1_{h0}")
            nc.vector.tensor_tensor(res[:], back[:, : h1 - h0], lasts[i][:], ADD)
            nc.sync.dma_start(out=out[P : 2 * P, h0:h1], in_=res[:])
